import numpy as np
import ml_dtypes


def mxq(x, axis, fmt="e4m3"):
    dtype, down = {"e4m3": (ml_dtypes.float8_e4m3fn, 7), "e5m2": (ml_dtypes.float8_e5m2, 14)}[fmt]
    v = np.moveaxis(np.asarray(x, np.float32).astype(ml_dtypes.bfloat16).astype(np.float64), axis, -1)
    blocks = v.reshape(v.shape[:-1] + (-1, 32))
    amax = np.abs(blocks).max(-1, keepdims=True)
    byte = np.maximum(np.where(amax > 0, np.frexp(amax)[1] - 1 + 127, 0) - down, 1)
    scale = np.exp2(byte - 127.0)
    codes = (blocks / scale).astype(np.float32).astype(dtype).astype(np.float64)
    return np.moveaxis((codes * scale).reshape(v.shape), -1, axis)


WIDE = False


def mx_kscale(k):
    if not WIDE:
        return np.ones(k)
    levels = np.array([10, -10, 5, -5, 0])
    if k % 512:
        return np.exp2(np.random.permutation(np.resize(levels, k // 32))).repeat(32)
    a = np.empty((k // 512, 16))
    for p in range(k // 512):
        a[p, :8] = np.random.permutation(np.resize(levels, 8))
        for g in range(8):
            far = levels[np.abs(levels - a[p, g]) >= 10]
            a[p, g + 8] = far[np.random.randint(len(far))]
    return np.exp2(a.ravel()).repeat(32)


def f64(x):
    return np.asarray(x).astype(np.float64)


def striped(idx):
    return np.tile(idx.reshape(-1, 16).T, (8, 1)).astype(np.uint16)


def unstriped(offs):
    return offs[:16].T.reshape(-1).astype(np.int64)


def relu(v):
    return np.maximum(v, 0.0)


K, T, S, H, N = 1024, 2048, 768, 512, 128


def setup_inputs():
    n = np.random.standard_normal
    s = mx_kscale(K)[:, None]
    u = mx_kscale(H)
    return {
        "xT": (n((K, T)) * s).astype(np.float32),
        "w1": (n((K, H)) / np.sqrt(K) / s).astype(np.float32),
        "w3": (n((K, H)) / np.sqrt(K) / s * u).astype(np.float32),
        "w2": (n((H, N)) / np.sqrt(H) / u[:, None]).astype(np.float32),
        "offs": striped(np.random.permutation(T)[:S]),
    }


def reference(xT, w1, w3, w2, offs):
    idx = unstriped(offs)
    xq = mxq(f64(xT)[:, idx], 0, "e4m3")
    h = relu(mxq(f64(w1), 0, "e4m3").T @ xq) * (mxq(f64(w3), 0, "e4m3").T @ xq)
    y = mxq(f64(w2), 0, "e4m3").T @ mxq(h, 0, "e4m3")
    return y

@@ -1,0 +1,203 @@
+from contextlib import ExitStack
+
+import concourse.mybir as mybir
+
+K, T, S, H, N = 1024, 2048, 768, 512, 128
+
+F32 = mybir.dt.float32
+BF16 = mybir.dt.bfloat16
+U32 = mybir.dt.uint32
+U16 = mybir.dt.uint16
+U8 = mybir.dt.uint8
+FP8X4 = mybir.dt.float8_e4m3fn_x4
+RELU = mybir.ActivationFunctionType.Relu
+MULT = mybir.AluOpType.mult
+
+P = 128
+PACK = 4
+K_PASS = P * PACK
+PASSES = K // K_PASS
+CHUNK = 128
+CHUNKS = S // CHUNK
+
+FLOPS = 2 * S * (2 * K * H + H * N)
+
+
+def tile_picked_pick_glu_relu_sub_e_kernel(tc, xT, w1, w3, w2, offs, out):
+    nc = tc.nc
+
+    with ExitStack() as ctx:
+        lists = ctx.enter_context(tc.tile_pool(name="lists", bufs=1))
+        keep = ctx.enter_context(tc.tile_pool(name="keep", bufs=1))
+        work = ctx.enter_context(tc.tile_pool(name="work", bufs=3))
+        psum = ctx.enter_context(tc.psum_pool(name="psum", bufs=3))
+
+        offsets = lists.tile([P, S // 16], U16, name="offsets")
+        nc.sync.dma_start(offsets[:], offs)
+
+        x_rows = xT.rearrange("(s p j) n -> s j p n", s=PASSES, j=PACK)
+        table = [[keep.tile([P, T], F32, name=f"table{s}{j}") for j in range(PACK)] for s in range(PASSES)]
+        raw1 = [keep.tile([P, PACK, H], F32, name=f"raw1_{s}") for s in range(PASSES)]
+        raw3 = [keep.tile([P, PACK, H], F32, name=f"raw3_{s}") for s in range(PASSES)]
+        raw2 = keep.tile([P, PACK, N], F32, name="raw2")
+        w1_rows = w1.rearrange("(s p j) c -> s p j c", s=PASSES, j=PACK)
+        w3_rows = w3.rearrange("(s p j) c -> s p j c", s=PASSES, j=PACK)
+        for j in range(PACK):
+            nc.sync.dma_start(table[0][j][:], x_rows[0, j])
+        nc.sync.dma_start(raw2[:], w2.rearrange("(p j) c -> p j c", j=PACK))
+        for j in range(PACK):
+            nc.sync.dma_start(table[1][j][:], x_rows[1, j])
+        nc.sync.dma_start(raw1[0][:], w1_rows[0])
+        nc.sync.dma_start(raw1[1][:], w1_rows[1])
+        nc.sync.dma_start(raw3[0][:], w3_rows[0])
+        nc.sync.dma_start(raw3[1][:, :, : H // 2], w3_rows[1][:, :, : H // 2])
+        nc.sync.dma_start(raw3[1][:, :, H // 2 :], w3_rows[1][:, :, H // 2 :])
+
+        picked = [keep.tile([P, PACK, S], F32, name=f"picked{s}") for s in range(PASSES)]
+        x_grouped = [keep.tile([P, S * PACK], BF16, name=f"xg{s}", align_bytes=64) for s in range(PASSES)]
+        x_codes = [keep.tile([P, S], U32, name=f"xc{s}", align_bytes=64) for s in range(PASSES)]
+        x_scales = [keep.tile([P, S], U8, name=f"xs{s}", align_bytes=64) for s in range(PASSES)]
+
+        def gather(s, j, a, b):
+            nc.vector.tensor_copy(picked[s][:, j, a:b], table[s][j][:].indirect(offsets[:, a // 16 : b // 16]))
+
+        def interleave(copy, s, a, b):
+            copy(
+                out=x_grouped[s][:, a * PACK : b * PACK].rearrange("p (c i t) -> p c t i", i=4, t=PACK),
+                in_=picked[s][:, :, a:b].rearrange("p t (c i) -> p c t i", i=4),
+            )
+
+        def quant_x(s, a, b):
+            nc.vector.quantize_mx(
+                out=x_codes[s][:, a:b].bitcast(FP8X4),
+                scales=x_scales[s][:, a:b],
+                in_=x_grouped[s][:, a * PACK : b * PACK],
+            )
+
+        def weight_tiles(name):
+            grouped = [keep.tile([P, H * PACK], BF16, name=f"{name}g{s}", align_bytes=64) for s in range(PASSES)]
+            codes = [keep.tile([P, H], U32, name=f"{name}c{s}", align_bytes=64) for s in range(PASSES)]
+            scales = [keep.tile([P, H], U8, name=f"{name}s{s}", align_bytes=64) for s in range(PASSES)]
+            return grouped, codes, scales
+
+        w1g, w1c, w1s = weight_tiles("w1")
+        w3g, w3c, w3s = weight_tiles("w3")
+
+        def cast_w(copy, grouped, raw, m0, m1):
+            copy(
+                out=grouped[:].rearrange("p (t m j) -> p m j t", t=PACK, j=PACK)[:, m0:m1],
+                in_=raw[:].rearrange("p j (m t) -> p m j t", t=PACK)[:, m0:m1],
+            )
+
+        def quant_w(grouped, codes, scales):
+            nc.vector.quantize_mx(out=codes[:].bitcast(FP8X4), scales=scales[:], in_=grouped[:])
+
+        def project(bank, codes, scales, c):
+            tok = slice(c * CHUNK, (c + 1) * CHUNK)
+            for t in range(PACK):
+                cols = slice(t * P, (t + 1) * P)
+                for s in range(PASSES):
+                    nc.tensor.matmul_mx(
+                        out=bank[:, t, :],
+                        lhsT=codes[s][:, cols].bitcast(FP8X4),
+                        lhsT_scale=scales[s][:, cols],
+                        rhs=x_codes[s][:, tok].bitcast(FP8X4),
+                        rhs_scale=x_scales[s][:, tok],
+                        start=(s == 0),
+                        stop=(s == PASSES - 1),
+                    )
+
+        vcopy = nc.vector.tensor_copy
+        scopy = nc.scalar.copy
+
+        for j in range(PACK):
+            gather(0, j, 0, S)
+        for a in range(0, S, 256):
+            interleave(scopy, 0, a, a + 256)
+
+        w2g = keep.tile([P, N * PACK], BF16, name="w2g", align_bytes=64)
+        w2c = keep.tile([P, N], U32, name="w2c", align_bytes=64)
+        w2s = keep.tile([P, N], U8, name="w2s", align_bytes=64)
+        scopy(
+            out=w2g[:].rearrange("p (c i j) -> p c j i", i=4, j=PACK),
+            in_=raw2[:].rearrange("p j (c i) -> p c j i", i=4),
+        )
+
+        gather(1, 0, 0, S)
+        quant_x(0, 0, 512)
+        quant_x(0, 512, S)
+        gather(1, 1, 0, S)
+        nc.vector.quantize_mx(out=w2c[:].bitcast(FP8X4), scales=w2s[:], in_=w2g[:])
+        gather(1, 2, 0, S)
+        gather(1, 3, 0, 256)
+        interleave(scopy, 1, 0, 256)
+        gather(1, 3, 256, 512)
+        interleave(scopy, 1, 256, 512)
+        gather(1, 3, 512, S)
+        cast_w(scopy, w1g[0], raw1[0], 0, 128)
+        interleave(vcopy, 1, 512, S)
+        quant_x(1, 0, 512)
+        quant_x(1, 512, S)
+        cast_w(scopy, w1g[1], raw1[1], 0, 64)
+        cast_w(vcopy, w1g[1], raw1[1], 64, 128)
+        quant_w(w1g[0], w1c[0], w1s[0])
+        quant_w(w1g[1], w1c[1], w1s[1])
+        cast_w(scopy, w3g[0], raw3[0], 0, 64)
+        cast_w(vcopy, w3g[0], raw3[0], 64, 128)
+        gates = []
+
+        def gate(c):
+            bank = psum.tile([P, PACK, CHUNK], F32, name="gate_bank")
+            project(bank, w1c, w1s, c)
+            r = keep.tile([P, CHUNK, PACK], F32, name=f"gate{c}")
+            nc.scalar.activation(out=r[:], in_=bank[:].rearrange("p t n -> p n t"), func=RELU)
+            gates.append(r)
+
+        gate(0)
+        gate(1)
+        quant_w(w3g[0], w3c[0], w3s[0])
+        cast_w(vcopy, w3g[1], raw3[1], 0, 64)
+        cast_w(vcopy, w3g[1], raw3[1], 64, 128)
+        quant_w(w3g[1], w3c[1], w3s[1])
+        for c in range(2, CHUNKS):
+            gate(c)
+
+        hidden = [None] * CHUNKS
+        result = keep.tile([P, S], F32, name="result")
+
+        def up(c):
+            bank = psum.tile([P, PACK, CHUNK], F32, name="up_bank")
+            project(bank, w3c, w3s, c)
+            hidden[c] = work.tile([P, CHUNK * PACK], BF16, name="hidden", align_bytes=64, bufs=6)
+            nc.vector.tensor_tensor(
+                out=hidden[c][:].rearrange("p (n t) -> p n t", t=PACK),
+                in0=bank[:].rearrange("p t n -> p n t"),
+                in1=gates[c][:],
+                op=MULT,
+            )
+
+        def down(c):
+            h_codes = work.tile([P, CHUNK], U32, name="h_codes", align_bytes=64)
+            h_scales = work.tile([P, CHUNK], U8, name="h_scales", align_bytes=64)
+            nc.vector.quantize_mx(out=h_codes[:].bitcast(FP8X4), scales=h_scales[:], in_=hidden[c][:])
+            y = psum.tile([P, CHUNK], F32, name="y_bank", bufs=2)
+            nc.tensor.matmul_mx(
+                out=y[:],
+                lhsT=w2c[:].bitcast(FP8X4),
+                lhsT_scale=w2s[:],
+                rhs=h_codes[:].bitcast(FP8X4),
+                rhs_scale=h_scales[:],
+                start=True,
+                stop=True,
+            )
+            tok = slice(c * CHUNK, (c + 1) * CHUNK)
+            nc.scalar.copy(out=result[:, tok], in_=y[:])
+            if c % 2 == 1:
+                pair = slice((c - 1) * CHUNK, (c + 1) * CHUNK)
+                nc.sync.dma_start(out[:, pair], result[:, pair])
+
+        up(0)
+        for c in range(1, CHUNKS):
+            up(c)
+            down(c - 1)
+        down(CHUNKS - 1)

@@ -44,7 +44,6 @@ def tile_picked_pick_glu_relu_sub_e_kernel(tc, xT, w1, w3, w2, offs, out):
         w3_rows = w3.rearrange("(s p j) c -> s p j c", s=PASSES, j=PACK)
         for j in range(PACK):
             nc.sync.dma_start(table[0][j][:], x_rows[0, j])
-        nc.sync.dma_start(raw2[:], w2.rearrange("(p j) c -> p j c", j=PACK))
         for j in range(PACK):
             nc.sync.dma_start(table[1][j][:], x_rows[1, j])
         nc.sync.dma_start(raw1[0][:], w1_rows[0])
@@ -52,6 +51,7 @@ def tile_picked_pick_glu_relu_sub_e_kernel(tc, xT, w1, w3, w2, offs, out):
         nc.sync.dma_start(raw3[0][:], w3_rows[0])
         nc.sync.dma_start(raw3[1][:, :, : H // 2], w3_rows[1][:, :, : H // 2])
         nc.sync.dma_start(raw3[1][:, :, H // 2 :], w3_rows[1][:, :, H // 2 :])
+        nc.sync.dma_start(raw2[:], w2.rearrange("(p j) c -> p j c", j=PACK))
 
         picked = [keep.tile([P, PACK, S], F32, name=f"picked{s}") for s in range(PASSES)]
         x_grouped = [keep.tile([P, S * PACK], BF16, name=f"xg{s}", align_bytes=64) for s in range(PASSES)]
@@ -92,6 +92,14 @@ def tile_picked_pick_glu_relu_sub_e_kernel(tc, xT, w1, w3, w2, offs, out):
         def quant_w(grouped, codes, scales):
             nc.vector.quantize_mx(out=codes[:].bitcast(FP8X4), scales=scales[:], in_=grouped[:])
 
+        def quant_w_half(grouped, codes, scales, half):
+            cols = slice(half * H // 2, (half + 1) * H // 2)
+            nc.vector.quantize_mx(
+                out=codes[:, cols].bitcast(FP8X4),
+                scales=scales[:, cols],
+                in_=grouped[:, half * H // 2 * PACK : (half + 1) * H // 2 * PACK],
+            )
+
         def project(bank, codes, scales, c):
             tok = slice(c * CHUNK, (c + 1) * CHUNK)
             for t in range(PACK):
@@ -110,68 +118,72 @@ def tile_picked_pick_glu_relu_sub_e_kernel(tc, xT, w1, w3, w2, offs, out):
         vcopy = nc.vector.tensor_copy
         scopy = nc.scalar.copy
 
-        for j in range(PACK):
+        for j in range(3):
             gather(0, j, 0, S)
         for a in range(0, S, 256):
+            gather(0, 3, a, a + 256)
             interleave(scopy, 0, a, a + 256)
-
-        w2g = keep.tile([P, N * PACK], BF16, name="w2g", align_bytes=64)
-        w2c = keep.tile([P, N], U32, name="w2c", align_bytes=64)
-        w2s = keep.tile([P, N], U8, name="w2s", align_bytes=64)
-        scopy(
-            out=w2g[:].rearrange("p (c i j) -> p c j i", i=4, j=PACK),
-            in_=raw2[:].rearrange("p j (c i) -> p c j i", i=4),
-        )
-
         gather(1, 0, 0, S)
-        quant_x(0, 0, 512)
-        quant_x(0, 512, S)
+        quant_x(0, 0, 256)
         gather(1, 1, 0, S)
-        nc.vector.quantize_mx(out=w2c[:].bitcast(FP8X4), scales=w2s[:], in_=w2g[:])
+        quant_x(0, 256, 512)
+        quant_x(0, 512, S)
         gather(1, 2, 0, S)
         gather(1, 3, 0, 256)
         interleave(scopy, 1, 0, 256)
         gather(1, 3, 256, 512)
         interleave(scopy, 1, 256, 512)
         gather(1, 3, 512, S)
-        cast_w(scopy, w1g[0], raw1[0], 0, 128)
+        cast_w(scopy, w1g[0], raw1[0], 0, 64)
         interleave(vcopy, 1, 512, S)
+        cast_w(vcopy, w1g[0], raw1[0], 64, 128)
         quant_x(1, 0, 512)
+        quant_w(w1g[0], w1c[0], w1s[0])
         quant_x(1, 512, S)
         cast_w(scopy, w1g[1], raw1[1], 0, 64)
         cast_w(vcopy, w1g[1], raw1[1], 64, 128)
-        quant_w(w1g[0], w1c[0], w1s[0])
         quant_w(w1g[1], w1c[1], w1s[1])
-        cast_w(scopy, w3g[0], raw3[0], 0, 64)
-        cast_w(vcopy, w3g[0], raw3[0], 64, 128)
+        w2g = keep.tile([P, N * PACK], BF16, name="w2g", align_bytes=64)
+        w2c = keep.tile([P, N], U32, name="w2c", align_bytes=64)
+        w2s = keep.tile([P, N], U8, name="w2s", align_bytes=64)
         gates = []
 
         def gate(c):
-            bank = psum.tile([P, PACK, CHUNK], F32, name="gate_bank")
+            bank = psum.tile([P, PACK, CHUNK], F32, name="bank", bufs=8)
             project(bank, w1c, w1s, c)
             r = keep.tile([P, CHUNK, PACK], F32, name=f"gate{c}")
             nc.scalar.activation(out=r[:], in_=bank[:].rearrange("p t n -> p n t"), func=RELU)
             gates.append(r)
 
-        gate(0)
-        gate(1)
+        for c in range(5):
+            gate(c)
+        cast_w(vcopy, w3g[0], raw3[0], 0, 128)
         quant_w(w3g[0], w3c[0], w3s[0])
         cast_w(vcopy, w3g[1], raw3[1], 0, 64)
         cast_w(vcopy, w3g[1], raw3[1], 64, 128)
-        quant_w(w3g[1], w3c[1], w3s[1])
-        for c in range(2, CHUNKS):
+        scopy(
+            out=w2g[:].rearrange("p (c i j) -> p c j i", i=4, j=PACK),
+            in_=raw2[:].rearrange("p j (c i) -> p c j i", i=4),
+        )
+        quant_w_half(w3g[1], w3c[1], w3s[1], 0)
+        quant_w_half(w3g[1], w3c[1], w3s[1], 1)
+        for c in range(5, CHUNKS):
             gate(c)
+        nc.vector.quantize_mx(out=w2c[:].bitcast(FP8X4), scales=w2s[:], in_=w2g[:])
 
         hidden = [None] * CHUNKS
+        banks = [None] * CHUNKS
         result = keep.tile([P, S], F32, name="result")
 
         def up(c):
-            bank = psum.tile([P, PACK, CHUNK], F32, name="up_bank")
-            project(bank, w3c, w3s, c)
+            banks[c] = psum.tile([P, PACK, CHUNK], F32, name="bank", bufs=8)
+            project(banks[c], w3c, w3s, c)
+
+        def multiply(c):
             hidden[c] = work.tile([P, CHUNK * PACK], BF16, name="hidden", align_bytes=64, bufs=6)
             nc.vector.tensor_tensor(
                 out=hidden[c][:].rearrange("p (n t) -> p n t", t=PACK),
-                in0=bank[:].rearrange("p t n -> p n t"),
+                in0=banks[c][:].rearrange("p t n -> p n t"),
                 in1=gates[c][:],
                 op=MULT,
             )
@@ -180,7 +192,7 @@ def tile_picked_pick_glu_relu_sub_e_kernel(tc, xT, w1, w3, w2, offs, out):
             h_codes = work.tile([P, CHUNK], U32, name="h_codes", align_bytes=64)
             h_scales = work.tile([P, CHUNK], U8, name="h_scales", align_bytes=64)
             nc.vector.quantize_mx(out=h_codes[:].bitcast(FP8X4), scales=h_scales[:], in_=hidden[c][:])
-            y = psum.tile([P, CHUNK], F32, name="y_bank", bufs=2)
+            y = psum.tile([P, CHUNK], F32, name="bank", bufs=8)
             nc.tensor.matmul_mx(
                 out=y[:],
                 lhsT=w2c[:].bitcast(FP8X4),
@@ -192,12 +204,38 @@ def tile_picked_pick_glu_relu_sub_e_kernel(tc, xT, w1, w3, w2, offs, out):
             )
             tok = slice(c * CHUNK, (c + 1) * CHUNK)
             nc.scalar.copy(out=result[:, tok], in_=y[:])
-            if c % 2 == 1:
-                pair = slice((c - 1) * CHUNK, (c + 1) * CHUNK)
+            if c in (1, 3, 4):
+                pair = slice(c // 2 * 2 * CHUNK, (c // 2 + 1) * 2 * CHUNK)
                 nc.sync.dma_start(out[:, pair], result[:, pair])
 
+        LAST = CHUNKS - 1
+
+        def multiply_gpsimd(c):
+            up_values = keep.tile([P, CHUNK, PACK], F32, name="up_values")
+            nc.scalar.copy(out=up_values[:], in_=banks[c][:].rearrange("p t n -> p n t"))
+            hidden[c] = work.tile([P, CHUNK * PACK], BF16, name="hidden", align_bytes=64, bufs=6)
+            nc.gpsimd.tensor_tensor(
+                out=hidden[c][:],
+                in0=up_values[:].rearrange("p n t -> p (n t)"),
+                in1=gates[c][:].rearrange("p n t -> p (n t)"),
+                op=MULT,
+            )
+
         up(0)
-        for c in range(1, CHUNKS):
-            up(c)
-            down(c - 1)
-        down(CHUNKS - 1)
+        up(LAST)
+        up(1)
+        up(2)
+        multiply_gpsimd(LAST)
+        multiply(0)
+        multiply(1)
+        up(3)
+        multiply(2)
+        down(0)
+        up(4)
+        multiply(3)
+        down(1)
+        down(2)
+        multiply(4)
+        down(3)
+        down(5)
+        down(4)

@@ -83,10 +83,10 @@ def tile_picked_pick_glu_relu_sub_e_kernel(tc, xT, w1, w3, w2, offs, out):
         w1g, w1c, w1s = weight_tiles("w1")
         w3g, w3c, w3s = weight_tiles("w3")
 
-        def cast_w(copy, grouped, raw, m0, m1):
+        def cast_w(copy, grouped, raw, m0, m1, t0=0, t1=PACK):
             copy(
-                out=grouped[:].rearrange("p (t m j) -> p m j t", t=PACK, j=PACK)[:, m0:m1],
-                in_=raw[:].rearrange("p j (m t) -> p m j t", t=PACK)[:, m0:m1],
+                out=grouped[:].rearrange("p (t m j) -> p m j t", t=PACK, j=PACK)[:, m0:m1, :, t0:t1],
+                in_=raw[:].rearrange("p j (m t) -> p m j t", t=PACK)[:, m0:m1, :, t0:t1],
             )
 
         def quant_w(grouped, codes, scales):
@@ -120,15 +120,15 @@ def tile_picked_pick_glu_relu_sub_e_kernel(tc, xT, w1, w3, w2, offs, out):
 
         for j in range(3):
             gather(0, j, 0, S)
+        gather(0, 3, 0, S)
         for a in range(0, S, 256):
-            gather(0, 3, a, a + 256)
             interleave(scopy, 0, a, a + 256)
         gather(1, 0, 0, S)
         quant_x(0, 0, 256)
         gather(1, 1, 0, S)
         quant_x(0, 256, 512)
-        quant_x(0, 512, S)
         gather(1, 2, 0, S)
+        quant_x(0, 512, S)
         gather(1, 3, 0, 256)
         interleave(scopy, 1, 0, 256)
         gather(1, 3, 256, 512)
@@ -160,7 +160,8 @@ def tile_picked_pick_glu_relu_sub_e_kernel(tc, xT, w1, w3, w2, offs, out):
         cast_w(vcopy, w3g[0], raw3[0], 0, 128)
         quant_w(w3g[0], w3c[0], w3s[0])
         cast_w(vcopy, w3g[1], raw3[1], 0, 64)
-        cast_w(vcopy, w3g[1], raw3[1], 64, 128)
+        cast_w(vcopy, w3g[1], raw3[1], 64, 128, 0, 2)
+        cast_w(vcopy, w3g[1], raw3[1], 64, 128, 2, 4)
         scopy(
             out=w2g[:].rearrange("p (c i j) -> p c j i", i=4, j=PACK),
             in_=raw2[:].rearrange("p j (c i) -> p c j i", i=4),
@@ -179,20 +180,40 @@ def tile_picked_pick_glu_relu_sub_e_kernel(tc, xT, w1, w3, w2, offs, out):
             banks[c] = psum.tile([P, PACK, CHUNK], F32, name="bank", bufs=8)
             project(banks[c], w3c, w3s, c)
 
-        def multiply(c):
-            hidden[c] = work.tile([P, CHUNK * PACK], BF16, name="hidden", align_bytes=64, bufs=6)
+        hidden_tiles = {}
+        def hidden_tile(group):
+            if group not in hidden_tiles:
+                hidden_tiles[group] = keep.tile([P, len(group) * CHUNK * PACK], BF16, name=f"hidden{group[0]}", align_bytes=64)
+            return hidden_tiles[group]
+
+        def multiply(c, group):
+            h = hidden_tile(group)
+            a = (c - group[0]) * CHUNK * PACK
             nc.vector.tensor_tensor(
-                out=hidden[c][:].rearrange("p (n t) -> p n t", t=PACK),
+                out=h[:, a : a + CHUNK * PACK].rearrange("p (n t) -> p n t", t=PACK),
                 in0=banks[c][:].rearrange("p t n -> p n t"),
                 in1=gates[c][:],
                 op=MULT,
             )
 
-        def down(c):
-            h_codes = work.tile([P, CHUNK], U32, name="h_codes", align_bytes=64)
-            h_scales = work.tile([P, CHUNK], U8, name="h_scales", align_bytes=64)
-            nc.vector.quantize_mx(out=h_codes[:].bitcast(FP8X4), scales=h_scales[:], in_=hidden[c][:])
-            y = psum.tile([P, CHUNK], F32, name="bank", bufs=8)
+        def multiply_gpsimd(c, group):
+            h = hidden_tile(group)
+            up_values = keep.tile([P, CHUNK, PACK], F32, name="up_values")
+            nc.scalar.copy(out=up_values[:], in_=banks[c][:].rearrange("p t n -> p n t"))
+            nc.gpsimd.tensor_tensor(
+                out=h[:],
+                in0=up_values[:].rearrange("p n t -> p (n t)"),
+                in1=gates[c][:].rearrange("p n t -> p (n t)"),
+                op=MULT,
+            )
+
+        def down(group):
+            n = len(group) * CHUNK
+            tok = slice(group[0] * CHUNK, group[0] * CHUNK + n)
+            h_codes = keep.tile([P, n], U32, name=f"h_codes{group[0]}", align_bytes=64)
+            h_scales = keep.tile([P, n], U8, name=f"h_scales{group[0]}", align_bytes=64)
+            nc.vector.quantize_mx(out=h_codes[:].bitcast(FP8X4), scales=h_scales[:], in_=hidden_tiles[group][:])
+            y = psum.tile([P, n], F32, name="bank", bufs=8)
             nc.tensor.matmul_mx(
                 out=y[:],
                 lhsT=w2c[:].bitcast(FP8X4),
@@ -202,40 +223,27 @@ def tile_picked_pick_glu_relu_sub_e_kernel(tc, xT, w1, w3, w2, offs, out):
                 start=True,
                 stop=True,
             )
-            tok = slice(c * CHUNK, (c + 1) * CHUNK)
             nc.scalar.copy(out=result[:, tok], in_=y[:])
-            if c in (1, 3, 4):
-                pair = slice(c // 2 * 2 * CHUNK, (c // 2 + 1) * 2 * CHUNK)
-                nc.sync.dma_start(out[:, pair], result[:, pair])
 
-        LAST = CHUNKS - 1
-
-        def multiply_gpsimd(c):
-            up_values = keep.tile([P, CHUNK, PACK], F32, name="up_values")
-            nc.scalar.copy(out=up_values[:], in_=banks[c][:].rearrange("p t n -> p n t"))
-            hidden[c] = work.tile([P, CHUNK * PACK], BF16, name="hidden", align_bytes=64, bufs=6)
-            nc.gpsimd.tensor_tensor(
-                out=hidden[c][:],
-                in0=up_values[:].rearrange("p n t -> p (n t)"),
-                in1=gates[c][:].rearrange("p n t -> p (n t)"),
-                op=MULT,
-            )
+        def store(a, b):
+            nc.sync.dma_start(out[:, a * CHUNK : b * CHUNK], result[:, a * CHUNK : b * CHUNK])
 
         up(0)
-        up(LAST)
         up(1)
         up(2)
-        multiply_gpsimd(LAST)
-        multiply(0)
-        multiply(1)
         up(3)
-        multiply(2)
-        down(0)
+        multiply(0, (0, 1))
+        multiply(1, (0, 1))
         up(4)
-        multiply(3)
-        down(1)
-        down(2)
-        multiply(4)
-        down(3)
-        down(5)
-        down(4)
+        multiply(2, (2, 3))
+        down((0, 1))
+        store(0, 2)
+        up(5)
+        multiply(3, (2, 3))
+        multiply(4, (4,))
+        down((2, 3))
+        store(2, 4)
+        multiply(5, (5,))
+        down((4,))
+        down((5,))
+        store(4, 6)

from contextlib import ExitStack

import concourse.mybir as mybir

K, T, S, H, N = 1024, 2048, 768, 512, 128

F32 = mybir.dt.float32
BF16 = mybir.dt.bfloat16
U32 = mybir.dt.uint32
U16 = mybir.dt.uint16
U8 = mybir.dt.uint8
FP8X4 = mybir.dt.float8_e4m3fn_x4
RELU = mybir.ActivationFunctionType.Relu
MULT = mybir.AluOpType.mult

P = 128
PACK = 4
K_PASS = P * PACK
PASSES = K // K_PASS
CHUNK = 128
CHUNKS = S // CHUNK

FLOPS = 2 * S * (2 * K * H + H * N)


def tile_picked_pick_glu_relu_sub_e_kernel(tc, xT, w1, w3, w2, offs, out):
    nc = tc.nc

    with ExitStack() as ctx:
        lists = ctx.enter_context(tc.tile_pool(name="lists", bufs=1))
        keep = ctx.enter_context(tc.tile_pool(name="keep", bufs=1))
        work = ctx.enter_context(tc.tile_pool(name="work", bufs=3))
        psum = ctx.enter_context(tc.psum_pool(name="psum", bufs=3))

        offsets = lists.tile([P, S // 16], U16, name="offsets")
        nc.sync.dma_start(offsets[:], offs)

        x_rows = xT.rearrange("(s p j) n -> s j p n", s=PASSES, j=PACK)
        table = [[keep.tile([P, T], F32, name=f"table{s}{j}") for j in range(PACK)] for s in range(PASSES)]
        raw1 = [keep.tile([P, PACK, H], F32, name=f"raw1_{s}") for s in range(PASSES)]
        raw3 = [keep.tile([P, PACK, H], F32, name=f"raw3_{s}") for s in range(PASSES)]
        raw2 = keep.tile([P, PACK, N], F32, name="raw2")
        w1_rows = w1.rearrange("(s p j) c -> s p j c", s=PASSES, j=PACK)
        w3_rows = w3.rearrange("(s p j) c -> s p j c", s=PASSES, j=PACK)
        for j in range(PACK):
            nc.sync.dma_start(table[0][j][:], x_rows[0, j])
        for j in range(PACK):
            nc.sync.dma_start(table[1][j][:], x_rows[1, j])
        nc.sync.dma_start(raw1[0][:], w1_rows[0])
        nc.sync.dma_start(raw1[1][:], w1_rows[1])
        nc.sync.dma_start(raw3[0][:], w3_rows[0])
        nc.sync.dma_start(raw3[1][:, :, : H // 2], w3_rows[1][:, :, : H // 2])
        nc.sync.dma_start(raw3[1][:, :, H // 2 :], w3_rows[1][:, :, H // 2 :])
        nc.sync.dma_start(raw2[:], w2.rearrange("(p j) c -> p j c", j=PACK))

        picked = [keep.tile([P, PACK, S], F32, name=f"picked{s}") for s in range(PASSES)]
        x_grouped = [keep.tile([P, S * PACK], BF16, name=f"xg{s}", align_bytes=64) for s in range(PASSES)]
        x_codes = [keep.tile([P, S], U32, name=f"xc{s}", align_bytes=64) for s in range(PASSES)]
        x_scales = [keep.tile([P, S], U8, name=f"xs{s}", align_bytes=64) for s in range(PASSES)]

        def gather(s, j, a, b):
            nc.vector.tensor_copy(picked[s][:, j, a:b], table[s][j][:].indirect(offsets[:, a // 16 : b // 16]))

        def interleave(copy, s, a, b):
            copy(
                out=x_grouped[s][:, a * PACK : b * PACK].rearrange("p (c i t) -> p c t i", i=4, t=PACK),
                in_=picked[s][:, :, a:b].rearrange("p t (c i) -> p c t i", i=4),
            )

        def quant_x(s, a, b):
            nc.vector.quantize_mx(
                out=x_codes[s][:, a:b].bitcast(FP8X4),
                scales=x_scales[s][:, a:b],
                in_=x_grouped[s][:, a * PACK : b * PACK],
            )

        def weight_tiles(name):
            grouped = [keep.tile([P, H * PACK], BF16, name=f"{name}g{s}", align_bytes=64) for s in range(PASSES)]
            codes = [keep.tile([P, H], U32, name=f"{name}c{s}", align_bytes=64) for s in range(PASSES)]
            scales = [keep.tile([P, H], U8, name=f"{name}s{s}", align_bytes=64) for s in range(PASSES)]
            return grouped, codes, scales

        w1g, w1c, w1s = weight_tiles("w1")
        w3g, w3c, w3s = weight_tiles("w3")

        def cast_w(copy, grouped, raw, m0, m1, t0=0, t1=PACK):
            copy(
                out=grouped[:].rearrange("p (t m j) -> p m j t", t=PACK, j=PACK)[:, m0:m1, :, t0:t1],
                in_=raw[:].rearrange("p j (m t) -> p m j t", t=PACK)[:, m0:m1, :, t0:t1],
            )

        def quant_w(grouped, codes, scales):
            nc.vector.quantize_mx(out=codes[:].bitcast(FP8X4), scales=scales[:], in_=grouped[:])

        def quant_w_half(grouped, codes, scales, half):
            cols = slice(half * H // 2, (half + 1) * H // 2)
            nc.vector.quantize_mx(
                out=codes[:, cols].bitcast(FP8X4),
                scales=scales[:, cols],
                in_=grouped[:, half * H // 2 * PACK : (half + 1) * H // 2 * PACK],
            )

        def project(bank, codes, scales, c):
            tok = slice(c * CHUNK, (c + 1) * CHUNK)
            for t in range(PACK):
                cols = slice(t * P, (t + 1) * P)
                for s in range(PASSES):
                    nc.tensor.matmul_mx(
                        out=bank[:, t, :],
                        lhsT=codes[s][:, cols].bitcast(FP8X4),
                        lhsT_scale=scales[s][:, cols],
                        rhs=x_codes[s][:, tok].bitcast(FP8X4),
                        rhs_scale=x_scales[s][:, tok],
                        start=(s == 0),
                        stop=(s == PASSES - 1),
                    )

        vcopy = nc.vector.tensor_copy
        scopy = nc.scalar.copy

        for j in range(3):
            gather(0, j, 0, S)
        gather(0, 3, 0, S)
        for a in range(0, S, 256):
            interleave(scopy, 0, a, a + 256)
        gather(1, 0, 0, S)
        quant_x(0, 0, 256)
        gather(1, 1, 0, S)
        quant_x(0, 256, 512)
        gather(1, 2, 0, S)
        quant_x(0, 512, S)
        gather(1, 3, 0, 256)
        interleave(scopy, 1, 0, 256)
        gather(1, 3, 256, 512)
        interleave(scopy, 1, 256, 512)
        gather(1, 3, 512, S)
        cast_w(scopy, w1g[0], raw1[0], 0, 64)
        interleave(vcopy, 1, 512, S)
        cast_w(vcopy, w1g[0], raw1[0], 64, 128)
        quant_x(1, 0, 512)
        quant_w(w1g[0], w1c[0], w1s[0])
        quant_x(1, 512, S)
        cast_w(scopy, w1g[1], raw1[1], 0, 64)
        cast_w(vcopy, w1g[1], raw1[1], 64, 128)
        quant_w(w1g[1], w1c[1], w1s[1])
        w2g = keep.tile([P, N * PACK], BF16, name="w2g", align_bytes=64)
        w2c = keep.tile([P, N], U32, name="w2c", align_bytes=64)
        w2s = keep.tile([P, N], U8, name="w2s", align_bytes=64)
        gates = []

        def gate(c):
            bank = psum.tile([P, PACK, CHUNK], F32, name="bank", bufs=8)
            project(bank, w1c, w1s, c)
            r = keep.tile([P, CHUNK, PACK], F32, name=f"gate{c}")
            nc.scalar.activation(out=r[:], in_=bank[:].rearrange("p t n -> p n t"), func=RELU)
            gates.append(r)

        for c in range(5):
            gate(c)
        cast_w(vcopy, w3g[0], raw3[0], 0, 128)
        quant_w(w3g[0], w3c[0], w3s[0])
        cast_w(vcopy, w3g[1], raw3[1], 0, 64)
        cast_w(vcopy, w3g[1], raw3[1], 64, 128, 0, 2)
        cast_w(vcopy, w3g[1], raw3[1], 64, 128, 2, 4)
        scopy(
            out=w2g[:].rearrange("p (c i j) -> p c j i", i=4, j=PACK),
            in_=raw2[:].rearrange("p j (c i) -> p c j i", i=4),
        )
        quant_w_half(w3g[1], w3c[1], w3s[1], 0)
        quant_w_half(w3g[1], w3c[1], w3s[1], 1)
        for c in range(5, CHUNKS):
            gate(c)
        nc.vector.quantize_mx(out=w2c[:].bitcast(FP8X4), scales=w2s[:], in_=w2g[:])

        hidden = [None] * CHUNKS
        banks = [None] * CHUNKS
        result = keep.tile([P, S], F32, name="result")

        def up(c):
            banks[c] = psum.tile([P, PACK, CHUNK], F32, name="bank", bufs=8)
            project(banks[c], w3c, w3s, c)

        hidden_tiles = {}
        def hidden_tile(group):
            if group not in hidden_tiles:
                hidden_tiles[group] = keep.tile([P, len(group) * CHUNK * PACK], BF16, name=f"hidden{group[0]}", align_bytes=64)
            return hidden_tiles[group]

        def multiply(c, group):
            h = hidden_tile(group)
            a = (c - group[0]) * CHUNK * PACK
            nc.vector.tensor_tensor(
                out=h[:, a : a + CHUNK * PACK].rearrange("p (n t) -> p n t", t=PACK),
                in0=banks[c][:].rearrange("p t n -> p n t"),
                in1=gates[c][:],
                op=MULT,
            )

        def multiply_gpsimd(c, group):
            h = hidden_tile(group)
            up_values = keep.tile([P, CHUNK, PACK], F32, name="up_values")
            nc.scalar.copy(out=up_values[:], in_=banks[c][:].rearrange("p t n -> p n t"))
            nc.gpsimd.tensor_tensor(
                out=h[:],
                in0=up_values[:].rearrange("p n t -> p (n t)"),
                in1=gates[c][:].rearrange("p n t -> p (n t)"),
                op=MULT,
            )

        def down(group):
            n = len(group) * CHUNK
            tok = slice(group[0] * CHUNK, group[0] * CHUNK + n)
            h_codes = keep.tile([P, n], U32, name=f"h_codes{group[0]}", align_bytes=64)
            h_scales = keep.tile([P, n], U8, name=f"h_scales{group[0]}", align_bytes=64)
            nc.vector.quantize_mx(out=h_codes[:].bitcast(FP8X4), scales=h_scales[:], in_=hidden_tiles[group][:])
            y = psum.tile([P, n], F32, name="bank", bufs=8)
            nc.tensor.matmul_mx(
                out=y[:],
                lhsT=w2c[:].bitcast(FP8X4),
                lhsT_scale=w2s[:],
                rhs=h_codes[:].bitcast(FP8X4),
                rhs_scale=h_scales[:],
                start=True,
                stop=True,
            )
            nc.scalar.copy(out=result[:, tok], in_=y[:])

        def store(a, b):
            nc.sync.dma_start(out[:, a * CHUNK : b * CHUNK], result[:, a * CHUNK : b * CHUNK])

        up(0)
        up(1)
        up(2)
        up(3)
        multiply(0, (0, 1))
        multiply(1, (0, 1))
        up(4)
        multiply(2, (2, 3))
        down((0, 1))
        store(0, 2)
        up(5)
        multiply(3, (2, 3))
        multiply(4, (4,))
        down((2, 3))
        store(2, 4)
        multiply(5, (5,))
        down((4,))
        down((5,))
        store(4, 6)
